import numpy as np
import ml_dtypes


def mxq(x, axis, fmt="e4m3"):
    dtype, down = {"e4m3": (ml_dtypes.float8_e4m3fn, 7), "e5m2": (ml_dtypes.float8_e5m2, 14)}[fmt]
    v = np.moveaxis(np.asarray(x, np.float32).astype(ml_dtypes.bfloat16).astype(np.float64), axis, -1)
    blocks = v.reshape(v.shape[:-1] + (-1, 32))
    amax = np.abs(blocks).max(-1, keepdims=True)
    byte = np.maximum(np.where(amax > 0, np.frexp(amax)[1] - 1 + 127, 0) - down, 1)
    scale = np.exp2(byte - 127.0)
    codes = (blocks / scale).astype(np.float32).astype(dtype).astype(np.float64)
    return np.moveaxis((codes * scale).reshape(v.shape), -1, axis)


WIDE = False


def mx_kscale(k):
    if not WIDE:
        return np.ones(k)
    levels = np.array([10, -10, 5, -5, 0])
    if k % 512:
        return np.exp2(np.random.permutation(np.resize(levels, k // 32))).repeat(32)
    a = np.empty((k // 512, 16))
    for p in range(k // 512):
        a[p, :8] = np.random.permutation(np.resize(levels, 8))
        for g in range(8):
            far = levels[np.abs(levels - a[p, g]) >= 10]
            a[p, g + 8] = far[np.random.randint(len(far))]
    return np.exp2(a.ravel()).repeat(32)


def f64(x):
    return np.asarray(x).astype(np.float64)


def striped(idx):
    return np.tile(idx.reshape(-1, 16).T, (8, 1)).astype(np.uint16)


def unstriped(offs):
    return offs[:16].T.reshape(-1).astype(np.int64)


E2M1 = np.array([0.0, 0.5, 1.0, 1.5, 2.0, 3.0, 4.0, 6.0, -0.0, -0.5, -1.0, -1.5, -2.0, -3.0, -4.0, -6.0])


def pack_weight(w, fmt):
    k, n = w.shape
    w = f64(np.asarray(w, np.float32).astype(ml_dtypes.bfloat16)).reshape(k // 32, 32, n)
    amax = np.abs(w).max(1)
    if fmt == "e4m3":
        byte = np.frexp(amax)[1] - 1 + 127 - 7
    else:
        mant, ex = np.frexp(amax / 6.0)
        byte = np.where(mant > 0.5, ex, ex - 1) + 127
    byte = np.clip(np.where(amax > 0, byte, 1), 1, 254)
    scaled = (w * np.exp2(127.0 - byte)[:, None, :]).reshape(k, n).astype(np.float32)
    by_word = np.ascontiguousarray(scaled.reshape(k // 512, 128, 4, n).transpose(0, 1, 3, 2))
    if fmt == "e4m3":
        words = by_word.astype(ml_dtypes.float8_e4m3fn).view(np.uint8)
    else:
        c = by_word.astype(ml_dtypes.float4_e2m1fn).view(np.uint8) & 0xF
        words = (c[..., 0::2] | (c[..., 1::2] << 4)).reshape(k // 512, 128, 2 * n)
    return np.ascontiguousarray(words), np.ascontiguousarray(byte.astype(np.uint8).reshape(k // 512, 16, n))


def unpack_weight(words, scales, fmt):
    g, _, n = scales.shape
    words = np.ascontiguousarray(words).reshape(g, 128, n, -1)
    if fmt == "e4m3":
        vals = words.view(ml_dtypes.float8_e4m3fn).astype(np.float64)
    else:
        nib = np.empty((g, 128, n, 4), np.uint8)
        nib[..., 0::2] = words & 0xF
        nib[..., 1::2] = words >> 4
        vals = E2M1[nib]
    vals = vals * np.repeat(np.exp2(scales.astype(np.float64) - 127.0), 8, axis=1)[..., None]
    return vals.transpose(0, 1, 3, 2).reshape(g * 512, n)


def relu2(v):
    return np.maximum(v, 0.0) ** 2


K, T, E, C, H, N = 512, 640, 10, 128, 1024, 128


def by_expert(wq, xq):
    return np.concatenate([wq[e].T @ xq[:, e * C:(e + 1) * C] for e in range(E)], axis=1)


def setup_inputs():
    n = np.random.standard_normal
    s = mx_kscale(K)[:, None]
    u = mx_kscale(H)
    first = np.random.permutation(np.repeat(np.arange(E), T // E))
    second = (first + 1 + np.random.permutation(np.repeat(np.arange(E - 1), -(-T // (E - 1)))[:T])) % E
    while np.bincount(second, minlength=E).max() != T // E:
        load = np.bincount(second, minlength=E); hi, lo = int(load.argmax()), int(load.argmin())
        t = np.flatnonzero((second == hi) & (first != lo))[0]; second[t] = lo
    slot_token = np.empty(E * C, np.int64); pos = np.empty((2, T), np.int64); fill = np.zeros(E, np.int64)
    place = np.stack([np.random.permutation(C) for _ in range(E)])
    for r, deal in enumerate((first, second)):
        for t in np.random.permutation(T):
            e = deal[t]; j = e * C + place[e, fill[e]]; fill[e] += 1; slot_token[j] = t; pos[r, t] = j
    g = np.random.uniform(0.2, 0.8, T)
    x = pack_weight(n((K, T)) * s, "e4m3")
    return {
        "x_words": x[0],
        "x_scales": x[1],
        "w1": (n((E + 1, K, H)) / np.sqrt(K) / s[None] * u[None, None, :]).astype(np.float32),
        "w2": (n((E + 1, H, N)) / np.sqrt(H) / u[None, :, None] ** 2).astype(np.float32),
        "gate": np.stack([np.tile(g, (N, 1)), np.tile(1.0 - g, (N, 1))]).astype(np.float32),
        "offs": striped(slot_token),
        "pos1": striped(pos[0]),
        "pos2": striped(pos[1]),
    }


def reference(x_words, x_scales, w1, w2, gate, offs, pos1, pos2):
    idx = unstriped(offs)
    w1q, w2q = mxq(f64(w1), 1, "e4m3"), mxq(f64(w2), 1, "e4m3")
    xs = unpack_weight(x_words, x_scales, "e4m3")
    hs = relu2(w1q[E].T @ xs)
    ys = w2q[E].T @ mxq(hs, 0, "e4m3")
    xq = unpack_weight(x_words, x_scales, "e4m3")[:, idx]
    h = relu2(by_expert(w1q, xq))
    y = by_expert(w2q, mxq(h, 0, "e4m3"))
    return ys + f64(gate[0]) * y[:, unstriped(pos1)] + f64(gate[1]) * y[:, unstriped(pos2)]

@@ -1,0 +1,280 @@
+from contextlib import ExitStack
+
+import concourse.mybir as mybir
+
+K, T, E, C, H, N = 512, 640, 10, 128, 1024, 128
+FLOPS = 2 * (E * C + T) * (K * H + H * N)
+
+F32 = mybir.dt.float32
+BF16 = mybir.dt.bfloat16
+I32 = mybir.dt.int32
+U32 = mybir.dt.uint32
+U16 = mybir.dt.uint16
+U8 = mybir.dt.uint8
+FP8X4 = mybir.dt.float8_e4m3fn_x4
+ACT = mybir.ActivationFunctionType
+ALU = mybir.AluOpType
+
+P = 128
+PACK = 4
+PASS = P * PACK
+PASSES = H // PASS
+SHARED = E
+LAST = E - 1
+CHUNKS = T // C
+UNITS = CHUNKS * PASSES
+HEAD_UNITS = 2
+GATHER_EXPERTS = ((0, 3), (3, 6), (6, 8), (8, 10))
+OUT_PARTS = ((0, 3), (3, 5))
+
+
+def tile_moe_shr_mlp_relu2_kernel(
+    tc, x_words, x_scales, w1, w2, gate, offs, pos1, pos2, out
+):
+    nc = tc.nc
+    with ExitStack() as ctx:
+        keep = ctx.enter_context(tc.tile_pool(name="keep", bufs=1))
+        ring = ctx.enter_context(tc.tile_pool(name="ring", bufs=1))
+        psum = ctx.enter_context(tc.psum_pool(name="psum", bufs=1))
+
+        offs_sb = keep.tile([P, E * C // 16], U16, name="offs_sb")
+        pos1_sb = keep.tile([P, T // 16], U16, name="pos1_sb")
+        pos2_sb = keep.tile([P, T // 16], U16, name="pos2_sb")
+        tok_words = keep.tile([P, T], I32, name="tok_words", align_bytes=64)
+        tok_scales = keep.tile([P, T], U8, name="tok_scales", align_bytes=64)
+        gate_sb = keep.tile([P, 2, T], F32, name="gate_sb", align_bytes=64)
+        y_slots = keep.tile([P, E * C], F32, name="y_slots", align_bytes=64)
+
+        w1_raw = {}
+        w2_raw = {}
+        w1_bf = {}
+        w1_q = {}
+        w2_q = {}
+        h_q = {}
+        hs_bf = {}
+        hs_q = {}
+        second_in = {}
+        slot_q = {}
+
+        def slot(tag, shape, dtype):
+            return ring.tile(shape, dtype, name=tag, align_bytes=64)
+
+        def load_w1(e):
+            raw = slot("w1_whole_%d" % (e % 4), [P, PACK, H], F32)
+            nc.sync.dma_start(out=raw[:], in_=w1[e].rearrange("(p j) c -> p j c", j=PACK))
+            for a in range(PASSES):
+                w1_raw[e, a] = raw[:, :, a * PASS : (a + 1) * PASS]
+
+        def load_w1_pass(e, a):
+            raw = slot("w1_half_%d" % a, [P, PACK, PASS], F32)
+            rows = w1[e].rearrange("(p j) c -> p j c", j=PACK)
+            nc.sync.dma_start(out=raw[:], in_=rows[:, :, a * PASS : (a + 1) * PASS])
+            w1_raw[e, a] = raw[:]
+
+        def load_w2(first, count):
+            raw = slot("w2_raw_%d" % first, [P, count * PASSES, PACK * N], F32)
+            nc.sync.dma_start(
+                out=raw[:],
+                in_=w2[first : first + count].rearrange("e (a p j) n -> p (e a) (j n)", p=P, j=PACK),
+            )
+            for i in range(count):
+                w2_raw[first + i] = raw[:, i * PASSES : (i + 1) * PASSES, :]
+
+        def round_w1(e, a):
+            grouped = slot("w1_bf_%d_%d" % (a, e % 2), [P, PASS * PACK], BF16)
+            dst = grouped[:].rearrange("p (t m j) -> p m j t", t=PACK, j=PACK)
+            src = w1_raw[e, a].rearrange("p j (m t) -> p m j t", t=PACK)
+            if e == SHARED:
+                nc.scalar.activation(dst, src, ACT.Copy)
+            else:
+                nc.vector.tensor_copy(dst, src)
+            w1_bf[e, a] = grouped
+
+        def round_w2(e, grouped, on_vector):
+            for a in range(PASSES):
+                dst = grouped[:, a * PASS : (a + 1) * PASS].rearrange("p (c i j) -> p c j i", i=4, j=PACK)
+                src = w2_raw[e][:, a, :].rearrange("p (j c i) -> p c j i", j=PACK, i=4)
+                if on_vector:
+                    nc.vector.tensor_copy(dst, src)
+                else:
+                    nc.scalar.activation(dst, src, ACT.Copy)
+
+        def quantize(values, width, codes_tag, scales_tag):
+            codes = slot(codes_tag, [P, width], U32)
+            scales = slot(scales_tag, [P, width], U8)
+            nc.vector.quantize_mx(out=codes[:].bitcast(FP8X4), scales=scales[:], in_=values)
+            return codes, scales
+
+        def quantize_w1(e, a):
+            owner = "shared" if e == SHARED else str(e % 2)
+            w1_q[e, a] = quantize(
+                w1_bf[e, a][:], PASS, "w1_codes_%d_%s" % (a, owner), "w1_scales_%d_%d" % (a, e)
+            )
+
+        def first_layer_pass(e, a, words, scales, bank_tag, relu):
+            bank = psum.tile([P, PACK, C], F32, name=bank_tag)
+            codes, plane = w1_q[e, a]
+            for t in range(PACK):
+                nc.tensor.matmul_mx(
+                    out=bank[:, t, :],
+                    lhsT=codes[:, t * P : (t + 1) * P].bitcast(FP8X4),
+                    lhsT_scale=plane[:, t * P : (t + 1) * P],
+                    rhs=words.bitcast(FP8X4),
+                    rhs_scale=scales,
+                    start=True,
+                    stop=True,
+                )
+            nc.scalar.activation(
+                relu.rearrange("p (c t) -> p c t", t=PACK), bank[:].rearrange("p t c -> p c t"), ACT.Relu
+            )
+
+        def second_layer(e, h_passes, sums):
+            w_codes, w_plane = w2_q[e]
+            for a in range(PASSES):
+                h_codes, h_plane = h_passes[a]
+                nc.tensor.matmul_mx(
+                    out=sums,
+                    lhsT=w_codes[:, a * N : (a + 1) * N].bitcast(FP8X4),
+                    lhsT_scale=w_plane[:, a * N : (a + 1) * N],
+                    rhs=h_codes.bitcast(FP8X4),
+                    rhs_scale=h_plane,
+                    start=(a == 0),
+                    stop=(a == PASSES - 1),
+                )
+
+        def routed_second_layer(e):
+            bank = psum.tile([P, C], F32, name="y_bank")
+            second_layer(e, h_q[e], bank[:])
+            nc.scalar.activation(y_slots[:, e * C : (e + 1) * C], bank[:], ACT.Copy)
+
+        def shared_unit(u, relu_tag):
+            s, a = divmod(u, PASSES)
+            cols = slice(s * C, (s + 1) * C)
+            relu = slot(relu_tag, [P, PASS], F32)
+            first_layer_pass(SHARED, a, tok_words[:, cols], tok_scales[:, cols], "shared_bank", relu[:])
+            h = slot("hs_bf_%d" % (u % 2), [P, PASS], BF16)
+            nc.scalar.activation(h[:], relu[:], ACT.Square)
+            hs_bf[u] = h
+
+        def quantize_shared_unit(u, scales_tag):
+            codes, scales = quantize(hs_bf[u][:], C, "hs_codes_%d" % u, scales_tag)
+            hs_q[u] = (codes[:], scales[:])
+
+        def quantize_second_inputs(e):
+            codes, scales = quantize(
+                second_in[e][:], 2 * PASSES * C, "w1_bf_0_%d" % ((e + 1) % 2), "second_scales_%d" % (e % 2)
+            )
+            h_q[e] = [(codes[:, a * C : (a + 1) * C], scales[:, a * C : (a + 1) * C]) for a in range(PASSES)]
+            w2_q[e] = (codes[:, PASSES * C :], scales[:, PASSES * C :])
+
+        nc.vector.memset(tok_scales[:].bitcast(I32), 0)
+        nc.sync.dma_start(out=tok_words[:], in_=x_words[0].rearrange("p t r -> p (t r)").bitcast(I32))
+        nc.sync.dma_start(offs_sb[:], offs)
+        for q in range(4):
+            nc.scalar.dma_start(
+                out=tok_scales[32 * q : 32 * q + 4, :].bitcast(I32),
+                in_=x_scales[0, 4 * q : 4 * q + 4, :].bitcast(I32),
+            )
+        load_w1_pass(SHARED, 0)
+        load_w1_pass(SHARED, 1)
+        load_w1(0)
+        load_w2(0, 2)
+        load_w1(1)
+        nc.sync.dma_start(pos1_sb[:], pos1)
+        nc.sync.dma_start(pos2_sb[:], pos2)
+        load_w1(2)
+
+        for first, last in GATHER_EXPERTS:
+            width = (last - first) * C
+            entries = offs_sb[:, first * C // 16 : last * C // 16]
+            words = keep.tile([P, width], U32, name="slot_words_%d" % first, align_bytes=64)
+            plane = keep.tile([P, width], U8, name="slot_scales_%d" % first, align_bytes=64)
+            nc.vector.tensor_copy(words[:], tok_words[:].bitcast(U32).indirect(entries))
+            nc.vector.tensor_copy(plane[:], tok_scales[:].indirect(entries))
+            for e in range(first, last):
+                cols = slice((e - first) * C, (e - first + 1) * C)
+                slot_q[e] = (words[:, cols], plane[:, cols])
+
+        for a in range(PASSES):
+            round_w1(SHARED, a)
+        for a in range(PASSES):
+            quantize_w1(SHARED, a)
+        for u in range(HEAD_UNITS):
+            shared_unit(u, "relu_%d" % (u % 2))
+
+        for e in range(E):
+            ahead = e + 3
+            if ahead in (3, 5, 7):
+                load_w2(ahead - 1, 2)
+            if ahead < LAST:
+                load_w1(ahead)
+            elif ahead == LAST:
+                load_w1_pass(LAST, 0)
+                load_w1_pass(LAST, 1)
+                load_w2(LAST - 1, 1)
+                load_w2(LAST, 1)
+                nc.sync.dma_start(out=gate_sb[:], in_=gate.rearrange("g p t -> p g t"))
+                load_w2(SHARED, 1)
+
+            relu = slot("relu_%d" % (e % 2), [P, PASSES * PASS], F32)
+            for a in range(PASSES):
+                round_w1(e, a)
+            for a in range(PASSES):
+                quantize_w1(e, a)
+                first_layer_pass(
+                    e, a, *slot_q[e], "a_bank_%d_%d" % (a, e % 2), relu[:, a * PASS : (a + 1) * PASS]
+                )
+            if e < LAST:
+                second_in[e] = slot("second_in_%d" % (e % 2), [P, 2 * PASSES * PASS], BF16)
+                nc.scalar.activation(second_in[e][:, : PASSES * PASS], relu[:], ACT.Square)
+            else:
+                h_last = slot("h_last", [P, PASSES * PASS], BF16)
+                for a in range(PASSES):
+                    cols = slice(a * PASS, (a + 1) * PASS)
+                    nc.scalar.activation(h_last[:, cols], relu[:, cols], ACT.Square)
+            if e >= 1:
+                if e == LAST:
+                    round_w2(e - 1, second_in[e - 1][:, PASSES * PASS :], False)
+                quantize_second_inputs(e - 1)
+                routed_second_layer(e - 1)
+            if e == 0:
+                quantize_shared_unit(0, "w1_scales_0_0")
+                quantize_shared_unit(1, "w1_scales_1_0")
+            elif e + 1 < UNITS:
+                quantize_shared_unit(e + 1, "w1_scales_0_%d" % e)
+            if e < LAST - 1:
+                round_w2(e, second_in[e][:, PASSES * PASS :], False)
+            if e + HEAD_UNITS < UNITS:
+                shared_unit(e + HEAD_UNITS, "relu_%d" % (e % 2))
+
+        w2_last = slot("w2_last", [P, PASSES * PASS], BF16)
+        round_w2(LAST, w2_last, True)
+        codes, scales = quantize(w2_last[:], PASSES * N, "w2_last_codes", "w2_last_scales")
+        w2_q[LAST] = (codes, scales)
+        codes, scales = quantize(h_last[:], PASSES * C, "h_last_codes", "h_last_scales")
+        h_q[LAST] = [(codes[:, a * C : (a + 1) * C], scales[:, a * C : (a + 1) * C]) for a in range(PASSES)]
+        routed_second_layer(LAST)
+        w2_shared = slot("w2_shared", [P, PASSES * PASS], BF16)
+        round_w2(SHARED, w2_shared, False)
+        w2_q[SHARED] = quantize(w2_shared[:], PASSES * N, "w2_shared_codes", "w2_shared_scales")
+
+        for first, last in OUT_PARTS:
+            cols = slice(first * C, last * C)
+            entries = slice(first * C // 16, last * C // 16)
+            width = (last - first) * C
+            ys_bank = psum.tile([P, width], F32, name="ys_bank_%d" % first)
+            for s in range(first, last):
+                second_layer(
+                    SHARED,
+                    [hs_q[s * PASSES + a] for a in range(PASSES)],
+                    ys_bank[:, (s - first) * C : (s - first + 1) * C],
+                )
+            one = keep.tile([P, width], F32, name="first_choice_%d" % first, align_bytes=64)
+            two = keep.tile([P, width], F32, name="second_choice_%d" % first, align_bytes=64)
+            part = keep.tile([P, width], F32, name="partial_%d" % first, align_bytes=64)
+            total = keep.tile([P, width], F32, name="total_%d" % first, align_bytes=64)
+            nc.vector.tensor_tensor(one[:], y_slots[:].indirect(pos1_sb[:, entries]), gate_sb[:, 0, cols], ALU.mult)
+            nc.vector.tensor_tensor(two[:], y_slots[:].indirect(pos2_sb[:, entries]), gate_sb[:, 1, cols], ALU.mult)
+            nc.vector.tensor_tensor(part[:], ys_bank[:], one[:], ALU.add)
+            nc.vector.tensor_tensor(total[:], part[:], two[:], ALU.add)
+            nc.sync.dma_start(out=out[:, cols], in_=total[:])

@@ -23,9 +23,17 @@ SHARED = E
 LAST = E - 1
 CHUNKS = T // C
 UNITS = CHUNKS * PASSES
-HEAD_UNITS = 2
+HEAD_UNITS = 4
+RAW_SLOTS = 4
 GATHER_EXPERTS = ((0, 3), (3, 6), (6, 8), (8, 10))
 OUT_PARTS = ((0, 3), (3, 5))
+W2_GROUPS = ((0,2,6,1),(2,2,6,1),(4,2,7,0),(6,2,7,0),(8,1,8,1),(9,1,8,1),(10,1,8,0))
+HALVES = (10,)
+SCALAR_HALVES = {(10, 0): 2, (10, 1): 2}
+Y_BANKS = ((0, 4), (4, 8), (8, 10))
+W2_BF_TAGS = ("w1_bf_0_0", "w1_bf_1_0", "hs_bf_0", "w1_bf_1_1", "hs_bf_1", "hs_relu_0", "hs_relu_1", "w1_codes_0_shared", "w1_codes_1_shared")
+Y_TAGS = ("y_bank_0", "y_bank_1", "a_bank_0_0", "a_bank_1_0", "a_bank_0_1")
+Y_ON_VECTOR = (9,)
 
 
 def tile_moe_shr_mlp_relu2_kernel(
@@ -42,6 +50,7 @@ def tile_moe_shr_mlp_relu2_kernel(
         pos2_sb = keep.tile([P, T // 16], U16, name="pos2_sb")
         tok_words = keep.tile([P, T], I32, name="tok_words", align_bytes=64)
         tok_scales = keep.tile([P, T], U8, name="tok_scales", align_bytes=64)
+        scale_rows = keep.tile([P, T], U8, name="scale_rows", align_bytes=64)
         gate_sb = keep.tile([P, 2, T], F32, name="gate_sb", align_bytes=64)
         y_slots = keep.tile([P, E * C], F32, name="y_slots", align_bytes=64)
 
@@ -50,139 +59,128 @@ def tile_moe_shr_mlp_relu2_kernel(
         w1_bf = {}
         w1_q = {}
         w2_q = {}
+        h_bf = {}
         h_q = {}
         hs_bf = {}
         hs_q = {}
-        second_in = {}
         slot_q = {}
 
         def slot(tag, shape, dtype):
             return ring.tile(shape, dtype, name=tag, align_bytes=64)
 
+        def raw_tag(e):
+            return "w1_raw_%d" % ((e + 1) % (E + 1) % RAW_SLOTS)
+
+        def bf_tag(e, a):
+            if (a == 0 and 1 <= e < E) or (a == 1 and e in (1, 2, 4, 6)):
+                return "w1_bf_own_%d_%d" % (a, e)
+            return "w1_bf_%d_%d" % (a, e % 2)
+
         def load_w1(e):
-            raw = slot("w1_whole_%d" % (e % 4), [P, PACK, H], F32)
-            nc.sync.dma_start(out=raw[:], in_=w1[e].rearrange("(p j) c -> p j c", j=PACK))
-            for a in range(PASSES):
-                w1_raw[e, a] = raw[:, :, a * PASS : (a + 1) * PASS]
-
-        def load_w1_pass(e, a):
-            raw = slot("w1_half_%d" % a, [P, PACK, PASS], F32)
             rows = w1[e].rearrange("(p j) c -> p j c", j=PACK)
-            nc.sync.dma_start(out=raw[:], in_=rows[:, :, a * PASS : (a + 1) * PASS])
-            w1_raw[e, a] = raw[:]
-
-        def load_w2(first, count):
-            raw = slot("w2_raw_%d" % first, [P, count * PASSES, PACK * N], F32)
-            nc.sync.dma_start(
-                out=raw[:],
-                in_=w2[first : first + count].rearrange("e (a p j) n -> p (e a) (j n)", p=P, j=PACK),
-            )
-            for i in range(count):
-                w2_raw[first + i] = raw[:, i * PASSES : (i + 1) * PASSES, :]
-
-        def round_w1(e, a):
-            grouped = slot("w1_bf_%d_%d" % (a, e % 2), [P, PASS * PACK], BF16)
-            dst = grouped[:].rearrange("p (t m j) -> p m j t", t=PACK, j=PACK)
-            src = w1_raw[e, a].rearrange("p j (m t) -> p m j t", t=PACK)
-            if e == SHARED:
-                nc.scalar.activation(dst, src, ACT.Copy)
+            if e in HALVES:
+                raw = slot(raw_tag(e), [P, PASSES, PACK, PASS], F32)
+                for a in range(PASSES):
+                    nc.sync.dma_start(out=raw[:, a, :, :], in_=rows[:, :, a * PASS : (a + 1) * PASS])
+                    w1_raw[e, a] = raw[:, a, :, :]
             else:
-                nc.vector.tensor_copy(dst, src)
-            w1_bf[e, a] = grouped
+                raw = slot(raw_tag(e), [P, PACK, H], F32)
+                nc.sync.dma_start(out=raw[:], in_=rows)
+                for a in range(PASSES):
+                    w1_raw[e, a] = raw[:, :, a * PASS : (a + 1) * PASS]
 
-        def round_w2(e, grouped, on_vector):
-            for a in range(PASSES):
-                dst = grouped[:, a * PASS : (a + 1) * PASS].rearrange("p (c i j) -> p c j i", i=4, j=PACK)
-                src = w2_raw[e][:, a, :].rearrange("p (j c i) -> p c j i", j=PACK, i=4)
-                if on_vector:
-                    nc.vector.tensor_copy(dst, src)
-                else:
-                    nc.scalar.activation(dst, src, ACT.Copy)
+        def load_w2(host):
+            groups = [g for g in W2_GROUPS if g[2] == host]
+            raw = slot(raw_tag(host), [P, sum(g[1] for g in groups) * PASSES, PACK * N], F32)
+            at = 0
+            for first, count, unused, on_vector in groups:
+                part = raw[:, at : at + count * PASSES, :]
+                nc.sync.dma_start(
+                    out=part,
+                    in_=w2[first : first + count].rearrange("e (a p j) n -> p (e a) (j n)", p=P, j=PACK),
+                )
+                w2_raw[first] = part
+                at += count * PASSES
+
+        def round_w1_pass(e, a):
+            w1_bf[e, a] = slot(bf_tag(e, a), [P, PASS * PACK], BF16)
+            dst = w1_bf[e, a][:].rearrange("p (t m j) -> p m j t", t=PACK, j=PACK)
+            src = w1_raw[e, a].rearrange("p j (m t) -> p m j t", t=PACK)
+            split = PACK - 2 * SCALAR_HALVES.get((e, a), 0)
+            if split < PACK:
+                nc.scalar.activation(dst[:, :, :, split:], src[:, :, :, split:], ACT.Copy)
+            if split > 0:
+                nc.vector.tensor_copy(dst[:, :, :, :split], src[:, :, :, :split])
 
         def quantize(values, width, codes_tag, scales_tag):
             codes = slot(codes_tag, [P, width], U32)
             scales = slot(scales_tag, [P, width], U8)
             nc.vector.quantize_mx(out=codes[:].bitcast(FP8X4), scales=scales[:], in_=values)
-            return codes, scales
+            return [(codes[:, c : c + P], scales[:, c : c + P]) for c in range(0, width, P)]
 
         def quantize_w1(e, a):
             owner = "shared" if e == SHARED else str(e % 2)
             w1_q[e, a] = quantize(
-                w1_bf[e, a][:], PASS, "w1_codes_%d_%s" % (a, owner), "w1_scales_%d_%d" % (a, e)
+                w1_bf[e, a][:], PASS, "w1_codes_%d_%s" % (a, owner), "w1_scales_%d_%s" % (a, owner)
             )
 
-        def first_layer_pass(e, a, words, scales, bank_tag, relu):
+        def multiply(sums, stationary, moving, start, stop):
+            nc.tensor.matmul_mx(
+                out=sums,
+                lhsT=stationary[0].bitcast(FP8X4),
+                lhsT_scale=stationary[1],
+                rhs=moving[0].bitcast(FP8X4),
+                rhs_scale=moving[1],
+                start=start,
+                stop=stop,
+            )
+
+        def first_layer_pass(e, a, tokens, bank_tag, relu):
             bank = psum.tile([P, PACK, C], F32, name=bank_tag)
-            codes, plane = w1_q[e, a]
             for t in range(PACK):
-                nc.tensor.matmul_mx(
-                    out=bank[:, t, :],
-                    lhsT=codes[:, t * P : (t + 1) * P].bitcast(FP8X4),
-                    lhsT_scale=plane[:, t * P : (t + 1) * P],
-                    rhs=words.bitcast(FP8X4),
-                    rhs_scale=scales,
-                    start=True,
-                    stop=True,
-                )
+                multiply(bank[:, t, :], w1_q[e, a][t], tokens, True, True)
             nc.scalar.activation(
                 relu.rearrange("p (c t) -> p c t", t=PACK), bank[:].rearrange("p t c -> p c t"), ACT.Relu
             )
 
         def second_layer(e, h_passes, sums):
-            w_codes, w_plane = w2_q[e]
             for a in range(PASSES):
-                h_codes, h_plane = h_passes[a]
-                nc.tensor.matmul_mx(
-                    out=sums,
-                    lhsT=w_codes[:, a * N : (a + 1) * N].bitcast(FP8X4),
-                    lhsT_scale=w_plane[:, a * N : (a + 1) * N],
-                    rhs=h_codes.bitcast(FP8X4),
-                    rhs_scale=h_plane,
-                    start=(a == 0),
-                    stop=(a == PASSES - 1),
-                )
+                multiply(sums, w2_q[e][a], h_passes[a], a == 0, a == PASSES - 1)
 
-        def routed_second_layer(e):
-            bank = psum.tile([P, C], F32, name="y_bank")
-            second_layer(e, h_q[e], bank[:])
-            nc.scalar.activation(y_slots[:, e * C : (e + 1) * C], bank[:], ACT.Copy)
-
-        def shared_unit(u, relu_tag):
+        def shared_unit(u, bank_tag):
             s, a = divmod(u, PASSES)
             cols = slice(s * C, (s + 1) * C)
-            relu = slot(relu_tag, [P, PASS], F32)
-            first_layer_pass(SHARED, a, tok_words[:, cols], tok_scales[:, cols], "shared_bank", relu[:])
-            h = slot("hs_bf_%d" % (u % 2), [P, PASS], BF16)
-            nc.scalar.activation(h[:], relu[:], ACT.Square)
-            hs_bf[u] = h
+            relu = slot("hs_relu_%d" % (u % 2), [P, PASS], F32)
+            first_layer_pass(SHARED, a, (tok_words[:, cols], tok_scales[:, cols]), bank_tag, relu[:])
+            first = 0 if u < HEAD_UNITS else u - u % 2
+            if u == first:
+                count = HEAD_UNITS if u == 0 else 2
+                hs_bf[first] = slot("hs_bf_%d" % (first // 2 % 2), [P, count * PASS], BF16)
+            nc.scalar.activation(hs_bf[first][:, (u - first) * PASS : (u - first + 1) * PASS], relu[:], ACT.Square)
 
-        def quantize_shared_unit(u, scales_tag):
-            codes, scales = quantize(hs_bf[u][:], C, "hs_codes_%d" % u, scales_tag)
-            hs_q[u] = (codes[:], scales[:])
+        def quantize_shared_units(first, count, codes_tag):
+            parts = quantize(hs_bf[first][:], count * C, codes_tag, "hs_scales_%d" % first)
+            for i in range(count):
+                hs_q[first + i] = parts[i]
 
-        def quantize_second_inputs(e):
-            codes, scales = quantize(
-                second_in[e][:], 2 * PASSES * C, "w1_bf_0_%d" % ((e + 1) % 2), "second_scales_%d" % (e % 2)
-            )
-            h_q[e] = [(codes[:, a * C : (a + 1) * C], scales[:, a * C : (a + 1) * C]) for a in range(PASSES)]
-            w2_q[e] = (codes[:, PASSES * C :], scales[:, PASSES * C :])
+        def quantize_h(e, codes_tag):
+            h_q[e] = quantize(h_bf[e][:], PASSES * C, codes_tag, "h_scales_%d" % e)
 
         nc.vector.memset(tok_scales[:].bitcast(I32), 0)
         nc.sync.dma_start(out=tok_words[:], in_=x_words[0].rearrange("p t r -> p (t r)").bitcast(I32))
         nc.sync.dma_start(offs_sb[:], offs)
         for q in range(4):
-            nc.scalar.dma_start(
-                out=tok_scales[32 * q : 32 * q + 4, :].bitcast(I32),
-                in_=x_scales[0, 4 * q : 4 * q + 4, :].bitcast(I32),
+            rows = slice(32 * q, 32 * q + 4)
+            nc.sync.dma_start(
+                out=scale_rows[rows, :].bitcast(I32), in_=x_scales[0, 4 * q : 4 * q + 4, :].bitcast(I32)
             )
-        load_w1_pass(SHARED, 0)
-        load_w1_pass(SHARED, 1)
+            nc.vector.tensor_copy(tok_scales[rows, :].bitcast(I32), scale_rows[rows, :].bitcast(I32))
+        load_w1(SHARED)
         load_w1(0)
-        load_w2(0, 2)
-        load_w1(1)
         nc.sync.dma_start(pos1_sb[:], pos1)
         nc.sync.dma_start(pos2_sb[:], pos2)
-        load_w1(2)
+        for e in range(1, RAW_SLOTS - 1):
+            load_w1(e)
 
         for first, last in GATHER_EXPERTS:
             width = (last - first) * C
@@ -196,68 +194,68 @@ def tile_moe_shr_mlp_relu2_kernel(
                 slot_q[e] = (words[:, cols], plane[:, cols])
 
         for a in range(PASSES):
-            round_w1(SHARED, a)
+            round_w1_pass(SHARED, a)
         for a in range(PASSES):
             quantize_w1(SHARED, a)
+        load_w1(RAW_SLOTS - 1)
         for u in range(HEAD_UNITS):
-            shared_unit(u, "relu_%d" % (u % 2))
+            shared_unit(u, "a_bank_%d_%d" % (u % 2, u // 2))
 
         for e in range(E):
-            ahead = e + 3
-            if ahead in (3, 5, 7):
-                load_w2(ahead - 1, 2)
-            if ahead < LAST:
-                load_w1(ahead)
-            elif ahead == LAST:
-                load_w1_pass(LAST, 0)
-                load_w1_pass(LAST, 1)
-                load_w2(LAST - 1, 1)
-                load_w2(LAST, 1)
-                nc.sync.dma_start(out=gate_sb[:], in_=gate.rearrange("g p t -> p g t"))
-                load_w2(SHARED, 1)
-
-            relu = slot("relu_%d" % (e % 2), [P, PASSES * PASS], F32)
             for a in range(PASSES):
-                round_w1(e, a)
+                round_w1_pass(e, a)
+            if e + RAW_SLOTS < E:
+                load_w1(e + RAW_SLOTS)
+            elif any(g[2] == e for g in W2_GROUPS):
+                load_w2(e)
+            if e == LAST:
+                nc.sync.dma_start(out=gate_sb[:], in_=gate.rearrange("g p t -> p g t"))
+            relu = slot("relu_%d" % (e % 2), [P, PASSES * PASS], F32)
             for a in range(PASSES):
                 quantize_w1(e, a)
                 first_layer_pass(
-                    e, a, *slot_q[e], "a_bank_%d_%d" % (a, e % 2), relu[:, a * PASS : (a + 1) * PASS]
+                    e, a, slot_q[e], "a_bank_%d_%d" % (a, e % 2), relu[:, a * PASS : (a + 1) * PASS]
                 )
-            if e < LAST:
-                second_in[e] = slot("second_in_%d" % (e % 2), [P, 2 * PASSES * PASS], BF16)
-                nc.scalar.activation(second_in[e][:, : PASSES * PASS], relu[:], ACT.Square)
-            else:
-                h_last = slot("h_last", [P, PASSES * PASS], BF16)
-                for a in range(PASSES):
-                    cols = slice(a * PASS, (a + 1) * PASS)
-                    nc.scalar.activation(h_last[:, cols], relu[:, cols], ACT.Square)
+            h_bf[e] = slot("h_bf_%d" % (e % 2), [P, PASSES * PASS], BF16)
+            nc.scalar.activation(h_bf[e][:], relu[:], ACT.Square)
             if e >= 1:
-                if e == LAST:
-                    round_w2(e - 1, second_in[e - 1][:, PASSES * PASS :], False)
-                quantize_second_inputs(e - 1)
-                routed_second_layer(e - 1)
-            if e == 0:
-                quantize_shared_unit(0, "w1_scales_0_0")
-                quantize_shared_unit(1, "w1_scales_1_0")
-            elif e + 1 < UNITS:
-                quantize_shared_unit(e + 1, "w1_scales_0_%d" % e)
-            if e < LAST - 1:
-                round_w2(e, second_in[e][:, PASSES * PASS :], False)
+                quantize_h(e - 1, bf_tag(e, 0))
+            if e == 1:
+                quantize_shared_units(0, HEAD_UNITS, bf_tag(e, 1))
+            elif e in (2, 4, 6):
+                quantize_shared_units(e + 2, 2, bf_tag(e, 1))
             if e + HEAD_UNITS < UNITS:
-                shared_unit(e + HEAD_UNITS, "relu_%d" % (e % 2))
+                shared_unit(e + HEAD_UNITS, "a_bank_0_%d" % (e % 2))
 
-        w2_last = slot("w2_last", [P, PASSES * PASS], BF16)
-        round_w2(LAST, w2_last, True)
-        codes, scales = quantize(w2_last[:], PASSES * N, "w2_last_codes", "w2_last_scales")
-        w2_q[LAST] = (codes, scales)
-        codes, scales = quantize(h_last[:], PASSES * C, "h_last_codes", "h_last_scales")
-        h_q[LAST] = [(codes[:, a * C : (a + 1) * C], scales[:, a * C : (a + 1) * C]) for a in range(PASSES)]
-        routed_second_layer(LAST)
-        w2_shared = slot("w2_shared", [P, PASSES * PASS], BF16)
-        round_w2(SHARED, w2_shared, False)
-        w2_q[SHARED] = quantize(w2_shared[:], PASSES * N, "w2_shared_codes", "w2_shared_scales")
+        y_banks = {}
+        for index, (first, count, unused, on_vector) in enumerate(W2_GROUPS):
+            grouped = slot(W2_BF_TAGS[index], [P, count * PASSES * PASS], BF16)
+            dst = grouped[:].rearrange("p (a c i j) -> p a c j i", a=count * PASSES, i=4, j=PACK)
+            src = w2_raw[first].rearrange("p a (j c i) -> p a c j i", j=PACK, i=4)
+            if on_vector:
+                nc.vector.tensor_copy(dst, src)
+            else:
+                nc.scalar.copy(dst, src)
+            if index == 0:
+                quantize_h(LAST, "h_last_codes")
+            parts = quantize(grouped[:], count * PASSES * N, "w2_codes_%d" % first, "w2_scales_%d" % first)
+            for i in range(count):
+                w2_q[first + i] = parts[i * PASSES : (i + 1) * PASSES]
+            for e in range(first, min(first + count, E)):
+                number, (low, high) = [(i, r) for i, r in enumerate(Y_BANKS) if r[0] <= e < r[1]][0]
+                if low not in y_banks:
+                    y_banks[low] = psum.tile([P, (high - low) * C], F32, name=Y_TAGS[number])
+                second_layer(e, h_q[e], y_banks[low][:, (e - low) * C : (e - low + 1) * C])
+                if e == high - 1:
+                    cols = slice(low * C, high * C)
+                    if e in Y_ON_VECTOR:
+                        nc.vector.tensor_copy(y_slots[:, cols], y_banks[low][:])
+                    else:
+                        nc.scalar.activation(y_slots[:, cols], y_banks[low][:], ACT.Copy)
 
+        one = keep.tile([P, T], F32, name="first_choice", align_bytes=64)
+        nc.vector.tensor_tensor(one[:], y_slots[:].indirect(pos1_sb[:]), gate_sb[:, 0, :], ALU.mult)
+        parts = []
         for first, last in OUT_PARTS:
             cols = slice(first * C, last * C)
             entries = slice(first * C // 16, last * C // 16)
@@ -269,12 +267,16 @@ def tile_moe_shr_mlp_relu2_kernel(
                     [hs_q[s * PASSES + a] for a in range(PASSES)],
                     ys_bank[:, (s - first) * C : (s - first + 1) * C],
                 )
-            one = keep.tile([P, width], F32, name="first_choice_%d" % first, align_bytes=64)
             two = keep.tile([P, width], F32, name="second_choice_%d" % first, align_bytes=64)
-            part = keep.tile([P, width], F32, name="partial_%d" % first, align_bytes=64)
+            nc.vector.tensor_tensor(
+                two[:], y_slots[:].indirect(pos2_sb[:, entries]), gate_sb[:, 1, cols], ALU.mult
+            )
+            parts.append((first, cols, width, ys_bank, two))
+        routed = {}
+        for first, cols, width, ys_bank, two in parts:
+            routed[first] = keep.tile([P, width], F32, name="routed_%d" % first, align_bytes=64)
+            nc.vector.tensor_tensor(routed[first][:], one[:, cols], two[:], ALU.add)
+        for first, cols, width, ys_bank, two in parts:
             total = keep.tile([P, width], F32, name="total_%d" % first, align_bytes=64)
-            nc.vector.tensor_tensor(one[:], y_slots[:].indirect(pos1_sb[:, entries]), gate_sb[:, 0, cols], ALU.mult)
-            nc.vector.tensor_tensor(two[:], y_slots[:].indirect(pos2_sb[:, entries]), gate_sb[:, 1, cols], ALU.mult)
-            nc.vector.tensor_tensor(part[:], ys_bank[:], one[:], ALU.add)
-            nc.vector.tensor_tensor(total[:], part[:], two[:], ALU.add)
+            nc.vector.tensor_tensor(total[:], ys_bank[:], routed[first][:], ALU.add)
             nc.sync.dma_start(out=out[:, cols], in_=total[:])

@@ -27,12 +27,14 @@ HEAD_UNITS = 4
 RAW_SLOTS = 4
 GATHER_EXPERTS = ((0, 3), (3, 6), (6, 8), (8, 10))
 OUT_PARTS = ((0, 3), (3, 5))
-W2_GROUPS = ((0,2,6,1),(2,2,6,1),(4,2,7,0),(6,2,7,0),(8,1,8,1),(9,1,8,1),(10,1,8,0))
-HALVES = (10,)
-SCALAR_HALVES = {(10, 0): 2, (10, 1): 2}
-Y_BANKS = ((0, 4), (4, 8), (8, 10))
+W2_GROUPS = ((4,2,6,0),(6,1,6,1),(7,1,6,1),(8,1,7,1),(9,1,7,1),(10,1,8,0))
+HALVES = ()
+SCALAR_HALVES = {(10,0):2}
+Y_BANKS = ((0,4),(4,8),(8,9),(9,10))
 W2_BF_TAGS = ("w1_bf_0_0", "w1_bf_1_0", "hs_bf_0", "w1_bf_1_1", "hs_bf_1", "hs_relu_0", "hs_relu_1", "w1_codes_0_shared", "w1_codes_1_shared")
-Y_TAGS = ("y_bank_0", "y_bank_1", "a_bank_0_0", "a_bank_1_0", "a_bank_0_1")
+Y_TAGS = ("y_bank_0", "y_bank_1", "y_bank_0", "y_bank_1", "a_bank_0_0", "a_bank_1_0")
+EARLY = ((0,2,4,5),(2,2,7,9))
+SQUARE_BY_PASS = ()
 Y_ON_VECTOR = (9,)
 
 
@@ -51,7 +53,8 @@ def tile_moe_shr_mlp_relu2_kernel(
         tok_words = keep.tile([P, T], I32, name="tok_words", align_bytes=64)
         tok_scales = keep.tile([P, T], U8, name="tok_scales", align_bytes=64)
         scale_rows = keep.tile([P, T], U8, name="scale_rows", align_bytes=64)
-        gate_sb = keep.tile([P, 2, T], F32, name="gate_sb", align_bytes=64)
+        gate_first = ring.tile([P, T], F32, name="gate_first", align_bytes=64)
+        gate_second = keep.tile([P, T], F32, name="gate_second", align_bytes=64)
         y_slots = keep.tile([P, E * C], F32, name="y_slots", align_bytes=64)
 
         w1_raw = {}
@@ -95,12 +98,18 @@ def tile_moe_shr_mlp_relu2_kernel(
             at = 0
             for first, count, unused, on_vector in groups:
                 part = raw[:, at : at + count * PASSES, :]
-                nc.sync.dma_start(
-                    out=part,
-                    in_=w2[first : first + count].rearrange("e (a p j) n -> p (e a) (j n)", p=P, j=PACK),
-                )
+                rows = w2[first : first + count].rearrange("e (a p j) n -> p (e a) (j n)", p=P, j=PACK)
+                if first == LAST:
+                    for a in range(PASSES):
+                        nc.sync.dma_start(out=part[:, a, :], in_=rows[:, a, :])
+                else:
+                    nc.sync.dma_start(out=part, in_=rows)
                 w2_raw[first] = part
                 at += count * PASSES
+                if first == LAST:
+                    nc.sync.dma_start(out=gate_first[:], in_=gate[0])
+                if first == SHARED:
+                    nc.sync.dma_start(out=gate_second[:], in_=gate[1])
 
         def round_w1_pass(e, a):
             w1_bf[e, a] = slot(bf_tag(e, a), [P, PASS * PACK], BF16)
@@ -166,6 +175,55 @@ def tile_moe_shr_mlp_relu2_kernel(
         def quantize_h(e, codes_tag):
             h_q[e] = quantize(h_bf[e][:], PASSES * C, codes_tag, "h_scales_%d" % e)
 
+        y_banks = {}
+        early_bf = {}
+
+        def round_w2(first, count, tag, on_vector):
+            grouped = slot(tag, [P, count * PASSES * PASS], BF16)
+            dst = grouped[:].rearrange("p (a c i j) -> p a c j i", a=count * PASSES, i=4, j=PACK)
+            src = w2_raw[first].rearrange("p a (j c i) -> p a c j i", j=PACK, i=4)
+            if first == LAST:
+                for a in range(PASSES):
+                    nc.vector.tensor_copy(dst[:, a], src[:, a])
+            elif on_vector:
+                nc.vector.tensor_copy(dst, src)
+            else:
+                nc.scalar.copy(dst, src)
+            return grouped
+
+        def second_layer_group(first, count, grouped, codes_tag):
+            if first == LAST:
+                parts = []
+                for a in range(PASSES):
+                    parts += quantize(
+                        grouped[:, a * PASS : (a + 1) * PASS], N, "w2_last_codes_%d" % a, "w2_last_scales_%d" % a
+                    )
+            else:
+                parts = quantize(grouped[:], count * PASSES * N, codes_tag, "w2_scales_%d" % first)
+            for i in range(count):
+                w2_q[first + i] = parts[i * PASSES : (i + 1) * PASSES]
+            for e in range(first, min(first + count, E)):
+                number, (low, high) = [(i, r) for i, r in enumerate(Y_BANKS) if r[0] <= e < r[1]][0]
+                if low not in y_banks:
+                    y_banks[low] = psum.tile([P, (high - low) * C], F32, name=Y_TAGS[number])
+                second_layer(e, h_q[e], y_banks[low][:, (e - low) * C : (e - low + 1) * C])
+                if e == high - 1:
+                    cols = slice(low * C, high * C)
+                    if e in Y_ON_VECTOR:
+                        nc.vector.tensor_copy(y_slots[:, cols], y_banks[low][:])
+                    else:
+                        nc.scalar.activation(y_slots[:, cols], y_banks[low][:], ACT.Copy)
+
+        def load_early(after):
+            for first, count, behind, used in EARLY:
+                if behind == after:
+                    raw = slot("w2_early_%d" % (first // 2 % 2), [P, count * PASSES, PACK * N], F32)
+                    nc.sync.dma_start(
+                        out=raw[:],
+                        in_=w2[first : first + count].rearrange("e (a p j) n -> p (e a) (j n)", p=P, j=PACK),
+                    )
+                    w2_raw[first] = raw[:]
+
         nc.vector.memset(tok_scales[:].bitcast(I32), 0)
         nc.sync.dma_start(out=tok_words[:], in_=x_words[0].rearrange("p t r -> p (t r)").bitcast(I32))
         nc.sync.dma_start(offs_sb[:], offs)
@@ -181,6 +239,7 @@ def tile_moe_shr_mlp_relu2_kernel(
         nc.sync.dma_start(pos2_sb[:], pos2)
         for e in range(1, RAW_SLOTS - 1):
             load_w1(e)
+            load_early(e)
 
         for first, last in GATHER_EXPERTS:
             width = (last - first) * C
@@ -198,6 +257,7 @@ def tile_moe_shr_mlp_relu2_kernel(
         for a in range(PASSES):
             quantize_w1(SHARED, a)
         load_w1(RAW_SLOTS - 1)
+        load_early(RAW_SLOTS - 1)
         for u in range(HEAD_UNITS):
             shared_unit(u, "a_bank_%d_%d" % (u % 2, u // 2))
 
@@ -206,55 +266,52 @@ def tile_moe_shr_mlp_relu2_kernel(
                 round_w1_pass(e, a)
             if e + RAW_SLOTS < E:
                 load_w1(e + RAW_SLOTS)
+                load_early(e + RAW_SLOTS)
             elif any(g[2] == e for g in W2_GROUPS):
                 load_w2(e)
-            if e == LAST:
-                nc.sync.dma_start(out=gate_sb[:], in_=gate.rearrange("g p t -> p g t"))
             relu = slot("relu_%d" % (e % 2), [P, PASSES * PASS], F32)
+            h_bf[e] = slot("h_bf_%d" % (e % 2), [P, PASSES * PASS], BF16)
             for a in range(PASSES):
                 quantize_w1(e, a)
                 first_layer_pass(
                     e, a, slot_q[e], "a_bank_%d_%d" % (a, e % 2), relu[:, a * PASS : (a + 1) * PASS]
                 )
-            h_bf[e] = slot("h_bf_%d" % (e % 2), [P, PASSES * PASS], BF16)
-            nc.scalar.activation(h_bf[e][:], relu[:], ACT.Square)
+                if e in SQUARE_BY_PASS:
+                    cols = slice(a * PASS, (a + 1) * PASS)
+                    nc.scalar.activation(h_bf[e][:, cols], relu[:, cols], ACT.Square)
+            if e not in SQUARE_BY_PASS:
+                nc.scalar.activation(h_bf[e][:], relu[:], ACT.Square)
             if e >= 1:
                 quantize_h(e - 1, bf_tag(e, 0))
             if e == 1:
                 quantize_shared_units(0, HEAD_UNITS, bf_tag(e, 1))
             elif e in (2, 4, 6):
                 quantize_shared_units(e + 2, 2, bf_tag(e, 1))
+            for first, count, behind, used in EARLY:
+                if used == e:
+                    second_layer_group(first, count, early_bf[first], bf_tag(e, 1))
+                if used == e + 1:
+                    early_bf[first] = round_w2(first, count, "w2_bf_early", False)
             if e + HEAD_UNITS < UNITS:
                 shared_unit(e + HEAD_UNITS, "a_bank_0_%d" % (e % 2))
 
-        y_banks = {}
-        for index, (first, count, unused, on_vector) in enumerate(W2_GROUPS):
-            grouped = slot(W2_BF_TAGS[index], [P, count * PASSES * PASS], BF16)
-            dst = grouped[:].rearrange("p (a c i j) -> p a c j i", a=count * PASSES, i=4, j=PACK)
-            src = w2_raw[first].rearrange("p a (j c i) -> p a c j i", j=PACK, i=4)
-            if on_vector:
-                nc.vector.tensor_copy(dst, src)
-            else:
-                nc.scalar.copy(dst, src)
-            if index == 0:
-                quantize_h(LAST, "h_last_codes")
-            parts = quantize(grouped[:], count * PASSES * N, "w2_codes_%d" % first, "w2_scales_%d" % first)
-            for i in range(count):
-                w2_q[first + i] = parts[i * PASSES : (i + 1) * PASSES]
-            for e in range(first, min(first + count, E)):
-                number, (low, high) = [(i, r) for i, r in enumerate(Y_BANKS) if r[0] <= e < r[1]][0]
-                if low not in y_banks:
-                    y_banks[low] = psum.tile([P, (high - low) * C], F32, name=Y_TAGS[number])
-                second_layer(e, h_q[e], y_banks[low][:, (e - low) * C : (e - low + 1) * C])
-                if e == high - 1:
-                    cols = slice(low * C, high * C)
-                    if e in Y_ON_VECTOR:
-                        nc.vector.tensor_copy(y_slots[:, cols], y_banks[low][:])
-                    else:
-                        nc.scalar.activation(y_slots[:, cols], y_banks[low][:], ACT.Copy)
+        bf = {}
+        bf[4] = round_w2(4, 2, "w1_bf_0_0", False)
+        bf[6] = round_w2(6, 1, "w1_bf_1_0", True)
+        bf[7] = round_w2(7, 1, "hs_bf_0", True)
+        second_layer_group(6, 1, bf[6], "w2_codes_6")
+        second_layer_group(4, 2, bf[4], raw_tag(6))
+        bf[8] = round_w2(8, 1, "w1_bf_1_1", True)
+        second_layer_group(7, 1, bf[7], "w2_codes_7")
+        bf[9] = round_w2(9, 1, "hs_bf_1", True)
+        quantize_h(LAST, raw_tag(7))
+        second_layer_group(8, 1, bf[8], "w2_codes_8")
+        second_layer_group(9, 1, bf[9], "w2_codes_9")
+        grouped = round_w2(10, 1, "hs_relu_0", False)
 
         one = keep.tile([P, T], F32, name="first_choice", align_bytes=64)
-        nc.vector.tensor_tensor(one[:], y_slots[:].indirect(pos1_sb[:]), gate_sb[:, 0, :], ALU.mult)
+        nc.vector.tensor_tensor(one[:], y_slots[:].indirect(pos1_sb[:]), gate_first[:], ALU.mult)
+        second_layer_group(SHARED, 1, grouped, "gate_first")
         parts = []
         for first, last in OUT_PARTS:
             cols = slice(first * C, last * C)
@@ -269,7 +326,7 @@ def tile_moe_shr_mlp_relu2_kernel(
                 )
             two = keep.tile([P, width], F32, name="second_choice_%d" % first, align_bytes=64)
             nc.vector.tensor_tensor(
-                two[:], y_slots[:].indirect(pos2_sb[:, entries]), gate_sb[:, 1, cols], ALU.mult
+                two[:], y_slots[:].indirect(pos2_sb[:, entries]), gate_second[:, cols], ALU.mult
             )
             parts.append((first, cols, width, ys_bank, two))
         routed = {}

@@ -26,15 +26,16 @@ UNITS = CHUNKS * PASSES
 HEAD_UNITS = 4
 RAW_SLOTS = 4
 GATHER_EXPERTS = ((0, 3), (3, 6), (6, 8), (8, 10))
-OUT_PARTS = ((0, 3), (3, 5))
-W2_GROUPS = ((4,2,6,0),(6,1,6,1),(7,1,6,1),(8,1,7,1),(9,1,7,1),(10,1,8,0))
+OUT_PARTS = ((0,2),(3,5),(2,3))
+W2_GROUPS = ((0,1,-1,0),(1,1,-1,0),(2,1,-2,0),(3,1,-2,0),(4,1,6,0),(5,1,6,0),(6,1,7,0),(7,1,7,0),(8,1,8,0),(9,1,8,0),(10,1,9,0))
 HALVES = ()
 SCALAR_HALVES = {(10,0):2}
-Y_BANKS = ((0,4),(4,8),(8,9),(9,10))
+Y_BANKS = ((0,2),(2,6),(6,9),(9,10))
 W2_BF_TAGS = ("w1_bf_0_0", "w1_bf_1_0", "hs_bf_0", "w1_bf_1_1", "hs_bf_1", "hs_relu_0", "hs_relu_1", "w1_codes_0_shared", "w1_codes_1_shared")
 Y_TAGS = ("y_bank_0", "y_bank_1", "y_bank_0", "y_bank_1", "a_bank_0_0", "a_bank_1_0")
-EARLY = ((0,2,4,5),(2,2,7,9))
+EARLY = ()
 SQUARE_BY_PASS = ()
+W2_ON_SCALAR = (0,4,6)
 Y_ON_VECTOR = (9,)
 
 
@@ -88,13 +89,15 @@ def tile_moe_shr_mlp_relu2_kernel(
                     w1_raw[e, a] = raw[:, a, :, :]
             else:
                 raw = slot(raw_tag(e), [P, PACK, H], F32)
-                nc.sync.dma_start(out=raw[:], in_=rows)
+                nc.sync.dma_start(
+                    out=raw[:].rearrange("p j c -> p (j c)"), in_=w1[e].rearrange("(p j) c -> p (j c)", j=PACK)
+                )
                 for a in range(PASSES):
                     w1_raw[e, a] = raw[:, :, a * PASS : (a + 1) * PASS]
 
         def load_w2(host):
             groups = [g for g in W2_GROUPS if g[2] == host]
-            raw = slot(raw_tag(host), [P, sum(g[1] for g in groups) * PASSES, PACK * N], F32)
+            raw = slot(raw_tag(host) if host >= 0 else "w2_raw_%d" % -host, [P, sum(g[1] for g in groups) * PASSES, PACK * N], F32)
             at = 0
             for first, count, unused, on_vector in groups:
                 part = raw[:, at : at + count * PASSES, :]
@@ -191,6 +194,17 @@ def tile_moe_shr_mlp_relu2_kernel(
                 nc.scalar.copy(dst, src)
             return grouped
 
+        def round_w2_into(e, grouped, on_vector):
+            dst = grouped.rearrange("p (a c i j) -> p a c j i", a=PASSES, i=4, j=PACK)
+            src = w2_raw[e].rearrange("p a (j c i) -> p a c j i", j=PACK, i=4)
+            if e == LAST and True:
+                for a in range(PASSES):
+                    nc.vector.tensor_copy(dst[:, a], src[:, a])
+            elif on_vector:
+                nc.vector.tensor_copy(dst, src)
+            else:
+                nc.scalar.copy(dst, src)
+
         def second_layer_group(first, count, grouped, codes_tag):
             if first == LAST:
                 parts = []
@@ -266,7 +280,9 @@ def tile_moe_shr_mlp_relu2_kernel(
                 round_w1_pass(e, a)
             if e + RAW_SLOTS < E:
                 load_w1(e + RAW_SLOTS)
-                load_early(e + RAW_SLOTS)
+                if e + RAW_SLOTS == LAST:
+                    load_w2(-1)
+                    load_w2(-2)
             elif any(g[2] == e for g in W2_GROUPS):
                 load_w2(e)
             relu = slot("relu_%d" % (e % 2), [P, PASSES * PASS], F32)
@@ -295,19 +311,21 @@ def tile_moe_shr_mlp_relu2_kernel(
             if e + HEAD_UNITS < UNITS:
                 shared_unit(e + HEAD_UNITS, "a_bank_0_%d" % (e % 2))
 
-        bf = {}
-        bf[4] = round_w2(4, 2, "w1_bf_0_0", False)
-        bf[6] = round_w2(6, 1, "w1_bf_1_0", True)
-        bf[7] = round_w2(7, 1, "hs_bf_0", True)
-        second_layer_group(6, 1, bf[6], "w2_codes_6")
-        second_layer_group(4, 2, bf[4], raw_tag(6))
-        bf[8] = round_w2(8, 1, "w1_bf_1_1", True)
-        second_layer_group(7, 1, bf[7], "w2_codes_7")
-        bf[9] = round_w2(9, 1, "hs_bf_1", True)
-        quantize_h(LAST, raw_tag(7))
-        second_layer_group(8, 1, bf[8], "w2_codes_8")
-        second_layer_group(9, 1, bf[9], "w2_codes_9")
-        grouped = round_w2(10, 1, "hs_relu_0", False)
+        for first, tag in zip(range(0, LAST - 1, 2), ("w1_bf_0_0", "w1_bf_1_0", "hs_bf_0", "w1_bf_1_1")):
+            grouped = slot(tag, [P, 2, PASSES * PASS], BF16)
+            for i in range(2):
+                round_w2_into(first + i, grouped[:, i, :], first + i not in W2_ON_SCALAR)
+            if first == 4:
+                quantize_h(LAST, "h_last_codes")
+            second_layer_group(first, 2, grouped[:].rearrange("p e w -> p (e w)"), "w2_codes_%d" % first)
+        grouped = slot("hs_bf_1", [P, PASSES * PASS], BF16)
+        round_w2_into(LAST - 1, grouped[:], LAST - 1 not in W2_ON_SCALAR)
+        last_bf = slot("hs_relu_0", [P, PASSES * PASS], BF16)
+        round_w2_into(LAST, last_bf[:], True)
+        second_layer_group(LAST - 1, 1, grouped, "w2_codes_8")
+        second_layer_group(LAST, 1, last_bf, "w2_codes_9")
+        grouped = slot("hs_relu_1", [P, PASSES * PASS], BF16)
+        round_w2_into(SHARED, grouped[:], False)
 
         one = keep.tile([P, T], F32, name="first_choice", align_bytes=64)
         nc.vector.tensor_tensor(one[:], y_slots[:].indirect(pos1_sb[:]), gate_first[:], ALU.mult)
@@ -317,14 +335,14 @@ def tile_moe_shr_mlp_relu2_kernel(
             cols = slice(first * C, last * C)
             entries = slice(first * C // 16, last * C // 16)
             width = (last - first) * C
-            ys_bank = psum.tile([P, width], F32, name="ys_bank_%d" % first)
+            ys_bank = psum.tile([P, width], F32, name="a_bank_%d_%d" % (first % 2, first // 2 % 2))
             for s in range(first, last):
                 second_layer(
                     SHARED,
                     [hs_q[s * PASSES + a] for a in range(PASSES)],
                     ys_bank[:, (s - first) * C : (s - first + 1) * C],
                 )
-            two = keep.tile([P, width], F32, name="second_choice_%d" % first, align_bytes=64)
+            two = slot("hs_relu_1" if first == 3 else "second_choice_%d" % first, [P, width], F32)
             nc.vector.tensor_tensor(
                 two[:], y_slots[:].indirect(pos2_sb[:, entries]), gate_second[:, cols], ALU.mult
             )

@@ -27,7 +27,7 @@ HEAD_UNITS = 4
 RAW_SLOTS = 4
 GATHER_EXPERTS = ((0, 3), (3, 6), (6, 8), (8, 10))
 OUT_PARTS = ((0,2),(3,5),(2,3))
-W2_GROUPS = ((0,1,-1,0),(1,1,-1,0),(2,1,-2,0),(3,1,-2,0),(4,1,6,0),(5,1,6,0),(6,1,7,0),(7,1,7,0),(8,1,8,0),(9,1,8,0),(10,1,9,0))
+W2_GROUPS = ((0,4,-1,0),(4,2,6,0),(6,1,7,0),(7,1,7,0),(8,1,8,0),(9,1,8,0),(10,1,9,0))
 HALVES = ()
 SCALAR_HALVES = {(10,0):2}
 Y_BANKS = ((0,2),(2,6),(6,9),(9,10))
@@ -35,7 +35,7 @@ W2_BF_TAGS = ("w1_bf_0_0", "w1_bf_1_0", "hs_bf_0", "w1_bf_1_1", "hs_bf_1", "hs_r
 Y_TAGS = ("y_bank_0", "y_bank_1", "y_bank_0", "y_bank_1", "a_bank_0_0", "a_bank_1_0")
 EARLY = ()
 SQUARE_BY_PASS = ()
-W2_ON_SCALAR = (0,4,6)
+W2_ON_SCALAR = (4,6)
 Y_ON_VECTOR = (9,)
 
 
@@ -107,10 +107,13 @@ def tile_moe_shr_mlp_relu2_kernel(
                         nc.sync.dma_start(out=part[:, a, :], in_=rows[:, a, :])
                 else:
                     nc.sync.dma_start(out=part, in_=rows)
-                w2_raw[first] = part
+                for i in range(count):
+                    w2_raw[first + i] = part[:, i * PASSES : (i + 1) * PASSES, :]
                 at += count * PASSES
                 if first == LAST:
+                    nc.sync.dma_start(pos1_sb[:], pos1)
                     nc.sync.dma_start(out=gate_first[:], in_=gate[0])
+                    nc.sync.dma_start(pos2_sb[:], pos2)
                 if first == SHARED:
                     nc.sync.dma_start(out=gate_second[:], in_=gate[1])
 
@@ -249,8 +252,6 @@ def tile_moe_shr_mlp_relu2_kernel(
             nc.vector.tensor_copy(tok_scales[rows, :].bitcast(I32), scale_rows[rows, :].bitcast(I32))
         load_w1(SHARED)
         load_w1(0)
-        nc.sync.dma_start(pos1_sb[:], pos1)
-        nc.sync.dma_start(pos2_sb[:], pos2)
         for e in range(1, RAW_SLOTS - 1):
             load_w1(e)
             load_early(e)
@@ -282,7 +283,6 @@ def tile_moe_shr_mlp_relu2_kernel(
                 load_w1(e + RAW_SLOTS)
                 if e + RAW_SLOTS == LAST:
                     load_w2(-1)
-                    load_w2(-2)
             elif any(g[2] == e for g in W2_GROUPS):
                 load_w2(e)
             relu = slot("relu_%d" % (e % 2), [P, PASSES * PASS], F32)

from contextlib import ExitStack

import concourse.mybir as mybir

K, T, E, C, H, N = 512, 640, 10, 128, 1024, 128
FLOPS = 2 * (E * C + T) * (K * H + H * N)

F32 = mybir.dt.float32
BF16 = mybir.dt.bfloat16
I32 = mybir.dt.int32
U32 = mybir.dt.uint32
U16 = mybir.dt.uint16
U8 = mybir.dt.uint8
FP8X4 = mybir.dt.float8_e4m3fn_x4
ACT = mybir.ActivationFunctionType
ALU = mybir.AluOpType

P = 128
PACK = 4
PASS = P * PACK
PASSES = H // PASS
SHARED = E
LAST = E - 1
CHUNKS = T // C
UNITS = CHUNKS * PASSES
HEAD_UNITS = 4
RAW_SLOTS = 4
GATHER_EXPERTS = ((0, 3), (3, 6), (6, 8), (8, 10))
OUT_PARTS = ((0,2),(3,5),(2,3))
W2_GROUPS = ((0,4,-1,0),(4,2,6,0),(6,1,7,0),(7,1,7,0),(8,1,8,0),(9,1,8,0),(10,1,9,0))
HALVES = ()
SCALAR_HALVES = {(10,0):2}
Y_BANKS = ((0,2),(2,6),(6,9),(9,10))
W2_BF_TAGS = ("w1_bf_0_0", "w1_bf_1_0", "hs_bf_0", "w1_bf_1_1", "hs_bf_1", "hs_relu_0", "hs_relu_1", "w1_codes_0_shared", "w1_codes_1_shared")
Y_TAGS = ("y_bank_0", "y_bank_1", "y_bank_0", "y_bank_1", "a_bank_0_0", "a_bank_1_0")
EARLY = ()
SQUARE_BY_PASS = ()
W2_ON_SCALAR = (4,6)
Y_ON_VECTOR = (9,)


def tile_moe_shr_mlp_relu2_kernel(
    tc, x_words, x_scales, w1, w2, gate, offs, pos1, pos2, out
):
    nc = tc.nc
    with ExitStack() as ctx:
        keep = ctx.enter_context(tc.tile_pool(name="keep", bufs=1))
        ring = ctx.enter_context(tc.tile_pool(name="ring", bufs=1))
        psum = ctx.enter_context(tc.psum_pool(name="psum", bufs=1))

        offs_sb = keep.tile([P, E * C // 16], U16, name="offs_sb")
        pos1_sb = keep.tile([P, T // 16], U16, name="pos1_sb")
        pos2_sb = keep.tile([P, T // 16], U16, name="pos2_sb")
        tok_words = keep.tile([P, T], I32, name="tok_words", align_bytes=64)
        tok_scales = keep.tile([P, T], U8, name="tok_scales", align_bytes=64)
        scale_rows = keep.tile([P, T], U8, name="scale_rows", align_bytes=64)
        gate_first = ring.tile([P, T], F32, name="gate_first", align_bytes=64)
        gate_second = keep.tile([P, T], F32, name="gate_second", align_bytes=64)
        y_slots = keep.tile([P, E * C], F32, name="y_slots", align_bytes=64)

        w1_raw = {}
        w2_raw = {}
        w1_bf = {}
        w1_q = {}
        w2_q = {}
        h_bf = {}
        h_q = {}
        hs_bf = {}
        hs_q = {}
        slot_q = {}

        def slot(tag, shape, dtype):
            return ring.tile(shape, dtype, name=tag, align_bytes=64)

        def raw_tag(e):
            return "w1_raw_%d" % ((e + 1) % (E + 1) % RAW_SLOTS)

        def bf_tag(e, a):
            if (a == 0 and 1 <= e < E) or (a == 1 and e in (1, 2, 4, 6)):
                return "w1_bf_own_%d_%d" % (a, e)
            return "w1_bf_%d_%d" % (a, e % 2)

        def load_w1(e):
            rows = w1[e].rearrange("(p j) c -> p j c", j=PACK)
            if e in HALVES:
                raw = slot(raw_tag(e), [P, PASSES, PACK, PASS], F32)
                for a in range(PASSES):
                    nc.sync.dma_start(out=raw[:, a, :, :], in_=rows[:, :, a * PASS : (a + 1) * PASS])
                    w1_raw[e, a] = raw[:, a, :, :]
            else:
                raw = slot(raw_tag(e), [P, PACK, H], F32)
                nc.sync.dma_start(
                    out=raw[:].rearrange("p j c -> p (j c)"), in_=w1[e].rearrange("(p j) c -> p (j c)", j=PACK)
                )
                for a in range(PASSES):
                    w1_raw[e, a] = raw[:, :, a * PASS : (a + 1) * PASS]

        def load_w2(host):
            groups = [g for g in W2_GROUPS if g[2] == host]
            raw = slot(raw_tag(host) if host >= 0 else "w2_raw_%d" % -host, [P, sum(g[1] for g in groups) * PASSES, PACK * N], F32)
            at = 0
            for first, count, unused, on_vector in groups:
                part = raw[:, at : at + count * PASSES, :]
                rows = w2[first : first + count].rearrange("e (a p j) n -> p (e a) (j n)", p=P, j=PACK)
                if first == LAST:
                    for a in range(PASSES):
                        nc.sync.dma_start(out=part[:, a, :], in_=rows[:, a, :])
                else:
                    nc.sync.dma_start(out=part, in_=rows)
                for i in range(count):
                    w2_raw[first + i] = part[:, i * PASSES : (i + 1) * PASSES, :]
                at += count * PASSES
                if first == LAST:
                    nc.sync.dma_start(pos1_sb[:], pos1)
                    nc.sync.dma_start(out=gate_first[:], in_=gate[0])
                    nc.sync.dma_start(pos2_sb[:], pos2)
                if first == SHARED:
                    nc.sync.dma_start(out=gate_second[:], in_=gate[1])

        def round_w1_pass(e, a):
            w1_bf[e, a] = slot(bf_tag(e, a), [P, PASS * PACK], BF16)
            dst = w1_bf[e, a][:].rearrange("p (t m j) -> p m j t", t=PACK, j=PACK)
            src = w1_raw[e, a].rearrange("p j (m t) -> p m j t", t=PACK)
            split = PACK - 2 * SCALAR_HALVES.get((e, a), 0)
            if split < PACK:
                nc.scalar.activation(dst[:, :, :, split:], src[:, :, :, split:], ACT.Copy)
            if split > 0:
                nc.vector.tensor_copy(dst[:, :, :, :split], src[:, :, :, :split])

        def quantize(values, width, codes_tag, scales_tag):
            codes = slot(codes_tag, [P, width], U32)
            scales = slot(scales_tag, [P, width], U8)
            nc.vector.quantize_mx(out=codes[:].bitcast(FP8X4), scales=scales[:], in_=values)
            return [(codes[:, c : c + P], scales[:, c : c + P]) for c in range(0, width, P)]

        def quantize_w1(e, a):
            owner = "shared" if e == SHARED else str(e % 2)
            w1_q[e, a] = quantize(
                w1_bf[e, a][:], PASS, "w1_codes_%d_%s" % (a, owner), "w1_scales_%d_%s" % (a, owner)
            )

        def multiply(sums, stationary, moving, start, stop):
            nc.tensor.matmul_mx(
                out=sums,
                lhsT=stationary[0].bitcast(FP8X4),
                lhsT_scale=stationary[1],
                rhs=moving[0].bitcast(FP8X4),
                rhs_scale=moving[1],
                start=start,
                stop=stop,
            )

        def first_layer_pass(e, a, tokens, bank_tag, relu):
            bank = psum.tile([P, PACK, C], F32, name=bank_tag)
            for t in range(PACK):
                multiply(bank[:, t, :], w1_q[e, a][t], tokens, True, True)
            nc.scalar.activation(
                relu.rearrange("p (c t) -> p c t", t=PACK), bank[:].rearrange("p t c -> p c t"), ACT.Relu
            )

        def second_layer(e, h_passes, sums):
            for a in range(PASSES):
                multiply(sums, w2_q[e][a], h_passes[a], a == 0, a == PASSES - 1)

        def shared_unit(u, bank_tag):
            s, a = divmod(u, PASSES)
            cols = slice(s * C, (s + 1) * C)
            relu = slot("hs_relu_%d" % (u % 2), [P, PASS], F32)
            first_layer_pass(SHARED, a, (tok_words[:, cols], tok_scales[:, cols]), bank_tag, relu[:])
            first = 0 if u < HEAD_UNITS else u - u % 2
            if u == first:
                count = HEAD_UNITS if u == 0 else 2
                hs_bf[first] = slot("hs_bf_%d" % (first // 2 % 2), [P, count * PASS], BF16)
            nc.scalar.activation(hs_bf[first][:, (u - first) * PASS : (u - first + 1) * PASS], relu[:], ACT.Square)

        def quantize_shared_units(first, count, codes_tag):
            parts = quantize(hs_bf[first][:], count * C, codes_tag, "hs_scales_%d" % first)
            for i in range(count):
                hs_q[first + i] = parts[i]

        def quantize_h(e, codes_tag):
            h_q[e] = quantize(h_bf[e][:], PASSES * C, codes_tag, "h_scales_%d" % e)

        y_banks = {}
        early_bf = {}

        def round_w2(first, count, tag, on_vector):
            grouped = slot(tag, [P, count * PASSES * PASS], BF16)
            dst = grouped[:].rearrange("p (a c i j) -> p a c j i", a=count * PASSES, i=4, j=PACK)
            src = w2_raw[first].rearrange("p a (j c i) -> p a c j i", j=PACK, i=4)
            if first == LAST:
                for a in range(PASSES):
                    nc.vector.tensor_copy(dst[:, a], src[:, a])
            elif on_vector:
                nc.vector.tensor_copy(dst, src)
            else:
                nc.scalar.copy(dst, src)
            return grouped

        def round_w2_into(e, grouped, on_vector):
            dst = grouped.rearrange("p (a c i j) -> p a c j i", a=PASSES, i=4, j=PACK)
            src = w2_raw[e].rearrange("p a (j c i) -> p a c j i", j=PACK, i=4)
            if e == LAST and True:
                for a in range(PASSES):
                    nc.vector.tensor_copy(dst[:, a], src[:, a])
            elif on_vector:
                nc.vector.tensor_copy(dst, src)
            else:
                nc.scalar.copy(dst, src)

        def second_layer_group(first, count, grouped, codes_tag):
            if first == LAST:
                parts = []
                for a in range(PASSES):
                    parts += quantize(
                        grouped[:, a * PASS : (a + 1) * PASS], N, "w2_last_codes_%d" % a, "w2_last_scales_%d" % a
                    )
            else:
                parts = quantize(grouped[:], count * PASSES * N, codes_tag, "w2_scales_%d" % first)
            for i in range(count):
                w2_q[first + i] = parts[i * PASSES : (i + 1) * PASSES]
            for e in range(first, min(first + count, E)):
                number, (low, high) = [(i, r) for i, r in enumerate(Y_BANKS) if r[0] <= e < r[1]][0]
                if low not in y_banks:
                    y_banks[low] = psum.tile([P, (high - low) * C], F32, name=Y_TAGS[number])
                second_layer(e, h_q[e], y_banks[low][:, (e - low) * C : (e - low + 1) * C])
                if e == high - 1:
                    cols = slice(low * C, high * C)
                    if e in Y_ON_VECTOR:
                        nc.vector.tensor_copy(y_slots[:, cols], y_banks[low][:])
                    else:
                        nc.scalar.activation(y_slots[:, cols], y_banks[low][:], ACT.Copy)

        def load_early(after):
            for first, count, behind, used in EARLY:
                if behind == after:
                    raw = slot("w2_early_%d" % (first // 2 % 2), [P, count * PASSES, PACK * N], F32)
                    nc.sync.dma_start(
                        out=raw[:],
                        in_=w2[first : first + count].rearrange("e (a p j) n -> p (e a) (j n)", p=P, j=PACK),
                    )
                    w2_raw[first] = raw[:]

        nc.vector.memset(tok_scales[:].bitcast(I32), 0)
        nc.sync.dma_start(out=tok_words[:], in_=x_words[0].rearrange("p t r -> p (t r)").bitcast(I32))
        nc.sync.dma_start(offs_sb[:], offs)
        for q in range(4):
            rows = slice(32 * q, 32 * q + 4)
            nc.sync.dma_start(
                out=scale_rows[rows, :].bitcast(I32), in_=x_scales[0, 4 * q : 4 * q + 4, :].bitcast(I32)
            )
            nc.vector.tensor_copy(tok_scales[rows, :].bitcast(I32), scale_rows[rows, :].bitcast(I32))
        load_w1(SHARED)
        load_w1(0)
        for e in range(1, RAW_SLOTS - 1):
            load_w1(e)
            load_early(e)

        for first, last in GATHER_EXPERTS:
            width = (last - first) * C
            entries = offs_sb[:, first * C // 16 : last * C // 16]
            words = keep.tile([P, width], U32, name="slot_words_%d" % first, align_bytes=64)
            plane = keep.tile([P, width], U8, name="slot_scales_%d" % first, align_bytes=64)
            nc.vector.tensor_copy(words[:], tok_words[:].bitcast(U32).indirect(entries))
            nc.vector.tensor_copy(plane[:], tok_scales[:].indirect(entries))
            for e in range(first, last):
                cols = slice((e - first) * C, (e - first + 1) * C)
                slot_q[e] = (words[:, cols], plane[:, cols])

        for a in range(PASSES):
            round_w1_pass(SHARED, a)
        for a in range(PASSES):
            quantize_w1(SHARED, a)
        load_w1(RAW_SLOTS - 1)
        load_early(RAW_SLOTS - 1)
        for u in range(HEAD_UNITS):
            shared_unit(u, "a_bank_%d_%d" % (u % 2, u // 2))

        for e in range(E):
            for a in range(PASSES):
                round_w1_pass(e, a)
            if e + RAW_SLOTS < E:
                load_w1(e + RAW_SLOTS)
                if e + RAW_SLOTS == LAST:
                    load_w2(-1)
            elif any(g[2] == e for g in W2_GROUPS):
                load_w2(e)
            relu = slot("relu_%d" % (e % 2), [P, PASSES * PASS], F32)
            h_bf[e] = slot("h_bf_%d" % (e % 2), [P, PASSES * PASS], BF16)
            for a in range(PASSES):
                quantize_w1(e, a)
                first_layer_pass(
                    e, a, slot_q[e], "a_bank_%d_%d" % (a, e % 2), relu[:, a * PASS : (a + 1) * PASS]
                )
                if e in SQUARE_BY_PASS:
                    cols = slice(a * PASS, (a + 1) * PASS)
                    nc.scalar.activation(h_bf[e][:, cols], relu[:, cols], ACT.Square)
            if e not in SQUARE_BY_PASS:
                nc.scalar.activation(h_bf[e][:], relu[:], ACT.Square)
            if e >= 1:
                quantize_h(e - 1, bf_tag(e, 0))
            if e == 1:
                quantize_shared_units(0, HEAD_UNITS, bf_tag(e, 1))
            elif e in (2, 4, 6):
                quantize_shared_units(e + 2, 2, bf_tag(e, 1))
            for first, count, behind, used in EARLY:
                if used == e:
                    second_layer_group(first, count, early_bf[first], bf_tag(e, 1))
                if used == e + 1:
                    early_bf[first] = round_w2(first, count, "w2_bf_early", False)
            if e + HEAD_UNITS < UNITS:
                shared_unit(e + HEAD_UNITS, "a_bank_0_%d" % (e % 2))

        for first, tag in zip(range(0, LAST - 1, 2), ("w1_bf_0_0", "w1_bf_1_0", "hs_bf_0", "w1_bf_1_1")):
            grouped = slot(tag, [P, 2, PASSES * PASS], BF16)
            for i in range(2):
                round_w2_into(first + i, grouped[:, i, :], first + i not in W2_ON_SCALAR)
            if first == 4:
                quantize_h(LAST, "h_last_codes")
            second_layer_group(first, 2, grouped[:].rearrange("p e w -> p (e w)"), "w2_codes_%d" % first)
        grouped = slot("hs_bf_1", [P, PASSES * PASS], BF16)
        round_w2_into(LAST - 1, grouped[:], LAST - 1 not in W2_ON_SCALAR)
        last_bf = slot("hs_relu_0", [P, PASSES * PASS], BF16)
        round_w2_into(LAST, last_bf[:], True)
        second_layer_group(LAST - 1, 1, grouped, "w2_codes_8")
        second_layer_group(LAST, 1, last_bf, "w2_codes_9")
        grouped = slot("hs_relu_1", [P, PASSES * PASS], BF16)
        round_w2_into(SHARED, grouped[:], False)

        one = keep.tile([P, T], F32, name="first_choice", align_bytes=64)
        nc.vector.tensor_tensor(one[:], y_slots[:].indirect(pos1_sb[:]), gate_first[:], ALU.mult)
        second_layer_group(SHARED, 1, grouped, "gate_first")
        parts = []
        for first, last in OUT_PARTS:
            cols = slice(first * C, last * C)
            entries = slice(first * C // 16, last * C // 16)
            width = (last - first) * C
            ys_bank = psum.tile([P, width], F32, name="a_bank_%d_%d" % (first % 2, first // 2 % 2))
            for s in range(first, last):
                second_layer(
                    SHARED,
                    [hs_q[s * PASSES + a] for a in range(PASSES)],
                    ys_bank[:, (s - first) * C : (s - first + 1) * C],
                )
            two = slot("hs_relu_1" if first == 3 else "second_choice_%d" % first, [P, width], F32)
            nc.vector.tensor_tensor(
                two[:], y_slots[:].indirect(pos2_sb[:, entries]), gate_second[:, cols], ALU.mult
            )
            parts.append((first, cols, width, ys_bank, two))
        routed = {}
        for first, cols, width, ys_bank, two in parts:
            routed[first] = keep.tile([P, width], F32, name="routed_%d" % first, align_bytes=64)
            nc.vector.tensor_tensor(routed[first][:], one[:, cols], two[:], ALU.add)
        for first, cols, width, ys_bank, two in parts:
            total = keep.tile([P, width], F32, name="total_%d" % first, align_bytes=64)
            nc.vector.tensor_tensor(total[:], ys_bank[:], routed[first][:], ALU.add)
            nc.sync.dma_start(out=out[:, cols], in_=total[:])
